import numpy as np
import ml_dtypes


def mxq(x, axis, fmt="e4m3"):
    dtype, down = {"e4m3": (ml_dtypes.float8_e4m3fn, 7), "e5m2": (ml_dtypes.float8_e5m2, 14)}[fmt]
    v = np.moveaxis(np.asarray(x, np.float32).astype(ml_dtypes.bfloat16).astype(np.float64), axis, -1)
    blocks = v.reshape(v.shape[:-1] + (-1, 32))
    amax = np.abs(blocks).max(-1, keepdims=True)
    byte = np.maximum(np.where(amax > 0, np.frexp(amax)[1] - 1 + 127, 0) - down, 1)
    scale = np.exp2(byte - 127.0)
    codes = (blocks / scale).astype(np.float32).astype(dtype).astype(np.float64)
    return np.moveaxis((codes * scale).reshape(v.shape), -1, axis)


WIDE = False


def mx_kscale(k):
    if not WIDE:
        return np.ones(k)
    levels = np.array([10, -10, 5, -5, 0])
    if k % 512:
        return np.exp2(np.random.permutation(np.resize(levels, k // 32))).repeat(32)
    a = np.empty((k // 512, 16))
    for p in range(k // 512):
        a[p, :8] = np.random.permutation(np.resize(levels, 8))
        for g in range(8):
            far = levels[np.abs(levels - a[p, g]) >= 10]
            a[p, g + 8] = far[np.random.randint(len(far))]
    return np.exp2(a.ravel()).repeat(32)


def f64(x):
    return np.asarray(x).astype(np.float64)


def striped(idx):
    return np.tile(idx.reshape(-1, 16).T, (8, 1)).astype(np.uint16)


def unstriped(offs):
    return offs[:16].T.reshape(-1).astype(np.int64)


E2M1 = np.array([0.0, 0.5, 1.0, 1.5, 2.0, 3.0, 4.0, 6.0, -0.0, -0.5, -1.0, -1.5, -2.0, -3.0, -4.0, -6.0])


def pack_weight(w, fmt):
    k, n = w.shape
    w = f64(np.asarray(w, np.float32).astype(ml_dtypes.bfloat16)).reshape(k // 32, 32, n)
    amax = np.abs(w).max(1)
    if fmt == "e4m3":
        byte = np.frexp(amax)[1] - 1 + 127 - 7
    else:
        mant, ex = np.frexp(amax / 6.0)
        byte = np.where(mant > 0.5, ex, ex - 1) + 127
    byte = np.clip(np.where(amax > 0, byte, 1), 1, 254)
    scaled = (w * np.exp2(127.0 - byte)[:, None, :]).reshape(k, n).astype(np.float32)
    by_word = np.ascontiguousarray(scaled.reshape(k // 512, 128, 4, n).transpose(0, 1, 3, 2))
    if fmt == "e4m3":
        words = by_word.astype(ml_dtypes.float8_e4m3fn).view(np.uint8)
    else:
        c = by_word.astype(ml_dtypes.float4_e2m1fn).view(np.uint8) & 0xF
        words = (c[..., 0::2] | (c[..., 1::2] << 4)).reshape(k // 512, 128, 2 * n)
    return np.ascontiguousarray(words), np.ascontiguousarray(byte.astype(np.uint8).reshape(k // 512, 16, n))


def unpack_weight(words, scales, fmt):
    g, _, n = scales.shape
    words = np.ascontiguousarray(words).reshape(g, 128, n, -1)
    if fmt == "e4m3":
        vals = words.view(ml_dtypes.float8_e4m3fn).astype(np.float64)
    else:
        nib = np.empty((g, 128, n, 4), np.uint8)
        nib[..., 0::2] = words & 0xF
        nib[..., 1::2] = words >> 4
        vals = E2M1[nib]
    vals = vals * np.repeat(np.exp2(scales.astype(np.float64) - 127.0), 8, axis=1)[..., None]
    return vals.transpose(0, 1, 3, 2).reshape(g * 512, n)


def gelu(v):
    return 0.5 * v * (1.0 + np.tanh(np.sqrt(2.0 / np.pi) * (v + 0.044715 * v**3)))


K, H, T, S, S2, T2, T3, L = 1024, 1024, 2048, 1024, 512, 2048, 2048, 128

def setup_inputs():
    n = np.random.standard_normal
    s = mx_kscale(K)[:, None]
    u = mx_kscale(H)[:, None]
    tab_words, tab_scales = pack_weight(n((K, T)) * s, "e4m3")
    tab2_words, tab2_scales = pack_weight(n((H, T3)) / np.sqrt(H) / u, "e4m3")
    w4_words, w4_scales = pack_weight(n((K, S2)) / np.sqrt(K) / s, "e2m1")
    return {
        "tab_words": tab_words, "tab_scales": tab_scales,
        "tab2_words": tab2_words, "tab2_scales": tab2_scales,
        "w4_words": w4_words, "w4_scales": w4_scales,
        "w1": (n((K, H)) / np.sqrt(K) / s * u.T).astype(np.float32),
        "least": (0.7 * n(H) * u[:, 0]).astype(np.float32),
        "last": n((S2, S)).astype(np.float32),
        "member": np.exp(0.4 * n(S2)).astype(np.float32),
        "page1": n((S2, T2)).astype(np.float32),
        "wgo": np.exp(0.3 * n((L, S))).astype(np.float32),
        "offs": striped(np.random.permutation(T)[:S]),
        "offs2": striped(np.random.permutation(T3)[:S2]),
        "offs3": striped(np.random.permutation(T2)[:S]),
    }

def reference(tab_words, tab_scales, tab2_words, tab2_scales, w4_words, w4_scales,
              w1, least, last, member, page1, wgo, offs, offs2, offs3):
    v = unpack_weight(tab_words, tab_scales, "e4m3")[:, unstriped(offs)]
    v2 = unpack_weight(tab2_words, tab2_scales, "e4m3")[:, unstriped(offs2)]
    w4 = unpack_weight(w4_words, w4_scales, "e2m1")
    w1q = mxq(f64(w1), 0, "e4m3")
    h = np.maximum(w1q.T @ v, f64(least)[:, None])
    hq = mxq(h, 0, "e4m3")
    e = v2.T @ hq + w4.T @ v
    score = np.maximum(e, f64(last)) * f64(member)[:, None]
    out = f64(page1).copy()
    out[:, unstriped(offs3)] = np.tile(f64(wgo), (S2 // L, 1)) * score
    return out

@@ -1,0 +1,224 @@
+from contextlib import ExitStack
+
+import concourse.mybir as mybir
+
+K, H, T, S, S2, T2, T3 = 1024, 1024, 2048, 1024, 512, 2048, 2048
+FLOPS = 2 * K * H * S + 2 * H * S2 * S + 2 * K * S2 * S
+
+F32 = mybir.dt.float32
+BF16 = mybir.dt.bfloat16
+I32 = mybir.dt.int32
+U32 = mybir.dt.uint32
+U16 = mybir.dt.uint16
+U8 = mybir.dt.uint8
+FP8X4 = mybir.dt.float8_e4m3fn_x4
+FP4X4 = mybir.dt.float4_e2m1fn_x4
+MAX = mybir.AluOpType.max
+MULT = mybir.AluOpType.mult
+COPY = mybir.ActivationFunctionType.Copy
+
+P = 128
+PACK = 4
+PASS = P * PACK
+PASSES = 2
+HALF = 512
+HALVES = S // HALF
+CHUNK = 128
+CHUNKS = HALF // CHUNK
+ROW_TILES = S2 // P
+QUADS = 4
+LIST_COLS = HALF // 16
+
+
+def tile_list_squash_ladder_page_kernel(
+    tc, tab_words, tab_scales, tab2_words, tab2_scales, w4_words, w4_scales,
+    w1, least, last, member, page1, wgo, offs, offs2, offs3, out,
+):
+    nc = tc.nc
+    with ExitStack() as ctx:
+        keep = ctx.enter_context(tc.tile_pool(name="keep", bufs=1))
+        ring = ctx.enter_context(tc.tile_pool(name="ring", bufs=2))
+        psum_h = ctx.enter_context(tc.psum_pool(name="psum_h", bufs=6))
+        psum_e = ctx.enter_context(tc.psum_pool(name="psum_e", bufs=2))
+
+        def held(shape, dtype, name, tag=""):
+            return keep.tile(shape, dtype, name=name, tag=tag or name, align_bytes=64)
+
+        idx = held([P, S // 16], U16, "idx")
+        idx2 = held([P, S2 // 16], U16, "idx2")
+        idx3 = held([P, S // 16], U16, "idx3")
+        tab_w = [held([P, T], I32, f"tab_w{a}") for a in range(PASSES)]
+        tab2_w = [held([P, T3], I32, f"tab2_w{a}") for a in range(PASSES)]
+        tab_s = held([P, T], U8, "tab_s")
+        tab2_s = held([P, T3], U8, "tab2_s")
+        w4_w = held([P, PASSES, 2 * S2], U8, "w4_w")
+        w4_s = held([P, PASSES, S2], U8, "w4_s")
+        v_s_low = held([P, S], U8, "v_s_low")
+        w1_raw = {(a, b): held([P, PACK, PASS], F32, f"w1_raw{a}{b}") for b in range(PASSES) for a in range(PASSES)}
+        least_sb = held([P, PASSES, PACK], F32, "least_sb")
+        member_sb = held([P, ROW_TILES], F32, "member_sb")
+        wgo_sb = held([P, S], F32, "wgo_sb")
+        last_sb = [held([P, ROW_TILES, HALF], F32, f"last{g}") for g in range(HALVES)]
+        page = [held([P, T2], F32, f"page{i}") for i in range(ROW_TILES)]
+
+        for plane in (tab_s, tab2_s, w4_s, v_s_low):
+            nc.vector.memset(plane[:].bitcast(I32), 0)
+
+        def load_words(tile, words, a):
+            nc.sync.dma_start(tile[:], words[a].rearrange("p t i -> p (t i)").bitcast(I32))
+
+        def load_packed_scales(queue, tile, scales):
+            for q in range(QUADS):
+                queue.dma_start(
+                    tile[32 * q : 32 * q + 4 * PASSES, :].bitcast(I32),
+                    scales[:, 4 * q : 4 * q + 4, :].bitcast(I32),
+                )
+
+        def load_w1(a, b):
+            rows = w1[PASS * a : PASS * (a + 1), PASS * b : PASS * (b + 1)]
+            nc.sync.dma_start(w1_raw[a, b][:], rows.rearrange("(p j) r -> p j r", j=PACK))
+
+        def load_last(g):
+            cols = last[:, HALF * g : HALF * (g + 1)]
+            nc.sync.dma_start(last_sb[g][:], cols.rearrange("(i p) j -> p i j", p=P))
+
+        def load_page(i):
+            nc.sync.dma_start(page[i][:], page1[P * i : P * (i + 1), :])
+
+        v_w = {}
+
+        def gather_words(a, g):
+            v_w[a, g] = held([P, HALF], U32, f"v_w{a}{g}")
+            entries = idx[:, LIST_COLS * g : LIST_COLS * (g + 1)]
+            nc.vector.tensor_copy(v_w[a, g][:], tab_w[a][:].bitcast(U32).indirect(entries))
+
+        w1_c, w1_s = {}, {}
+
+        def round_w1(a, b, copy):
+            grouped = ring.tile([P, PASS * PACK], BF16, name="w1_grouped", align_bytes=64, bufs=4)
+            copy(
+                grouped[:].rearrange("p (t m j) -> p m t j", t=PACK, j=PACK),
+                w1_raw[a, b][:].rearrange("p j (m t) -> p m t j", t=PACK),
+            )
+            return grouped
+
+        def quantize_w1(a, b, grouped):
+            w1_c[a, b] = held([P, PASS], U32, f"w1_c{a}{b}")
+            w1_s[a, b] = held([P, PASS], U8, f"w1_s{a}{b}")
+            nc.vector.quantize_mx(out=w1_c[a, b][:].bitcast(FP8X4), scales=w1_s[a, b][:], in_=grouped[:])
+
+        v_s = held([P, S], U8, "v_s")
+        v2_w = [held([P, S2], U32, f"v2_w{a}") for a in range(PASSES)]
+        v2_s = held([P, S2], U8, "v2_s")
+        floor = held([P, PASSES, CHUNK, PACK], BF16, "floor")
+
+        nc.sync.dma_start(idx[:], offs)
+        nc.sync.dma_start(idx2[:], offs2)
+        load_w1(0, 0)
+        load_packed_scales(nc.sync, tab_s, tab_scales)
+        load_w1(1, 0)
+        load_packed_scales(nc.sync, tab2_s, tab2_scales)
+        load_words(tab_w[0], tab_words, 0)
+        load_words(tab_w[1], tab_words, 1)
+        nc.sync.dma_start(least_sb[:], least.rearrange("(b p t) -> p b t", b=PASSES, t=PACK))
+        load_w1(0, 1)
+        for q in range(QUADS):
+            nc.sync.dma_start(
+                w4_s[32 * q : 32 * q + 4, :, :].bitcast(I32),
+                w4_scales[:, 4 * q : 4 * q + 4, :].rearrange("a r c -> r a c").bitcast(I32),
+            )
+        load_w1(1, 1)
+        nc.vector.tensor_copy(v_s[:], tab_s[:].indirect(idx[:]))
+        nc.sync.dma_start(v_s_low[0:112, :].bitcast(I32), v_s[4:116, :].bitcast(I32))
+        load_words(tab2_w[0], tab2_words, 0)
+        load_words(tab2_w[1], tab2_words, 1)
+        nc.sync.dma_start(w4_w[:].bitcast(I32), w4_words.rearrange("a p c -> p a c").bitcast(I32))
+        nc.sync.dma_start(idx3[:], offs3)
+        with nc.allow_non_contiguous_dma(reason="one factor for each partition"):
+            nc.sync.dma_start(member_sb[:], member.rearrange("(i p) -> p i", p=P))
+        load_last(0)
+        nc.sync.dma_start(wgo_sb[:], wgo)
+        for i in range(ROW_TILES):
+            load_page(i)
+        load_last(1)
+
+        quantize_w1(0, 0, round_w1(0, 0, nc.scalar.copy))
+        nc.vector.tensor_copy(v2_s[:], tab2_s[:].indirect(idx2[:]))
+        quantize_w1(1, 0, round_w1(1, 0, nc.scalar.copy))
+        nc.scalar.copy(floor[:], least_sb[:].unsqueeze(2).to_broadcast([P, PASSES, CHUNK, PACK]))
+
+        for g in range(HALVES):
+            for a in range(PASSES):
+                gather_words(a, g)
+        quantize_w1(0, 1, round_w1(0, 1, nc.scalar.copy))
+        quantize_w1(1, 1, round_w1(1, 1, nc.vector.tensor_copy))
+        for a in range(PASSES):
+            nc.vector.tensor_copy(v2_w[a][:], tab2_w[a][:].bitcast(U32).indirect(idx2[:]))
+
+        h_c, h_s = {}, {}
+
+        def features(b, g):
+            h = held([P, CHUNKS, CHUNK * PACK], BF16, f"h{b}{g}", tag="w1_raw11" if (b, g) == (0, 0) else "")
+            for c in range(CHUNKS):
+                bank = psum_h.tile([P, PACK, CHUNK], F32, name="bank_h")
+                cols = slice(CHUNK * c, CHUNK * (c + 1))
+                list_cols = slice(HALF * g + CHUNK * c, HALF * g + CHUNK * (c + 1))
+                for t in range(PACK):
+                    slot = slice(P * t, P * (t + 1))
+                    for a in range(PASSES):
+                        nc.tensor.matmul_mx(
+                            out=bank[:, t, :],
+                            lhsT=w1_c[a, b][:, slot].bitcast(FP8X4),
+                            lhsT_scale=w1_s[a, b][:, slot],
+                            rhs=v_w[a, g][:, cols].bitcast(FP8X4),
+                            rhs_scale=v_s[4 * a : P, list_cols],
+                            start=(a == 0),
+                            stop=(a == PASSES - 1),
+                        )
+                nc.scalar.copy(h[:, c, :].rearrange("p (n t) -> p n t", t=PACK), bank[:].rearrange("p t n -> p n t"))
+            floors = floor[:, b, :, :].rearrange("p n t -> p (n t)").unsqueeze(1).to_broadcast([P, CHUNKS, CHUNK * PACK])
+            nc.vector.tensor_tensor(h[:], h[:], floors, MAX)
+            h_c[b, g] = held([P, HALF], U32, f"h_c{b}{g}")
+            h_s[b, g] = held([P, HALF], U8, f"h_s{b}{g}")
+            nc.vector.quantize_mx(
+                out=h_c[b, g][:].bitcast(FP8X4), scales=h_s[b, g][:], in_=h[:].rearrange("p c x -> p (c x)")
+            )
+
+        def place_scores(i, g):
+            cols = slice(HALF * g, HALF * (g + 1))
+            rows = slice(P * i, P * (i + 1))
+            bank = psum_e.tile([P, HALF], F32, name="bank_e")
+            for a in range(PASSES):
+                nc.tensor.matmul_mx(
+                    out=bank[:],
+                    lhsT=w4_w[:, a, 2 * P * i : 2 * P * (i + 1)].bitcast(FP4X4),
+                    lhsT_scale=w4_s[:, a, rows],
+                    rhs=v_w[a, g][:].bitcast(FP8X4),
+                    rhs_scale=(v_s, v_s_low)[a][:, cols],
+                    start=(a == 0),
+                    stop=False,
+                )
+            for b in range(PASSES):
+                nc.tensor.matmul_mx(
+                    out=bank[:],
+                    lhsT=v2_w[b][:, rows].bitcast(FP8X4),
+                    lhsT_scale=v2_s[4 * b : P, rows],
+                    rhs=h_c[b, g][:].bitcast(FP8X4),
+                    rhs_scale=h_s[b, g][:],
+                    start=False,
+                    stop=(b == PASSES - 1),
+                )
+            factor = ring.tile([P, HALF], F32, name="factor", bufs=8)
+            nc.scalar.activation(factor[:], wgo_sb[:, cols], COPY, scale=member_sb[:, i : i + 1])
+            best = ring.tile([P, HALF], F32, name="best", bufs=4)
+            nc.vector.tensor_tensor(best[:], bank[:], last_sb[g][:, i, :], MAX)
+            places = idx3[:, LIST_COLS * g : LIST_COLS * (g + 1)]
+            nc.vector.tensor_tensor(page[i][:].indirect(places), best[:], factor[:], MULT)
+            if g == HALVES - 1:
+                nc.sync.dma_start(out[rows, :], page[i][:])
+
+        for g in range(HALVES):
+            for b in range(PASSES):
+                features(b, g)
+            for i in range(ROW_TILES):
+                place_scores(i, g)

@@ -28,6 +28,7 @@ CHUNKS = HALF // CHUNK
 ROW_TILES = S2 // P
 QUADS = 4
 LIST_COLS = HALF // 16
+FLOOR_RUN = 32
 
 
 def tile_list_squash_ladder_page_kernel(
@@ -57,8 +58,8 @@ def tile_list_squash_ladder_page_kernel(
         w1_raw = {(a, b): held([P, PACK, PASS], F32, f"w1_raw{a}{b}") for b in range(PASSES) for a in range(PASSES)}
         least_sb = held([P, PASSES, PACK], F32, "least_sb")
         member_sb = held([P, ROW_TILES], F32, "member_sb")
-        wgo_sb = held([P, S], F32, "wgo_sb")
-        last_sb = [held([P, ROW_TILES, HALF], F32, f"last{g}") for g in range(HALVES)]
+        wgo_sb = [held([P, HALF], F32, f"wgo{g}") for g in range(HALVES)]
+        last_sb = {(i, g): held([P, HALF], F32, f"last{i}{g}") for g in range(HALVES) for i in range(ROW_TILES)}
         page = [held([P, T2], F32, f"page{i}") for i in range(ROW_TILES)]
 
         for plane in (tab_s, tab2_s, w4_s, v_s_low):
@@ -78,9 +79,11 @@ def tile_list_squash_ladder_page_kernel(
             rows = w1[PASS * a : PASS * (a + 1), PASS * b : PASS * (b + 1)]
             nc.sync.dma_start(w1_raw[a, b][:], rows.rearrange("(p j) r -> p j r", j=PACK))
 
-        def load_last(g):
-            cols = last[:, HALF * g : HALF * (g + 1)]
-            nc.sync.dma_start(last_sb[g][:], cols.rearrange("(i p) j -> p i j", p=P))
+        def load_last(i, g):
+            nc.sync.dma_start(last_sb[i, g][:], last[P * i : P * (i + 1), HALF * g : HALF * (g + 1)])
+
+        def load_wgo(g):
+            nc.sync.dma_start(wgo_sb[g][:], wgo[:, HALF * g : HALF * (g + 1)])
 
         def load_page(i):
             nc.sync.dma_start(page[i][:], page1[P * i : P * (i + 1), :])
@@ -94,12 +97,13 @@ def tile_list_squash_ladder_page_kernel(
 
         w1_c, w1_s = {}, {}
 
-        def round_w1(a, b, copy):
+        def round_w1(a, b, scalar_share):
             grouped = ring.tile([P, PASS * PACK], BF16, name="w1_grouped", align_bytes=64, bufs=4)
-            copy(
-                grouped[:].rearrange("p (t m j) -> p m t j", t=PACK, j=PACK),
-                w1_raw[a, b][:].rearrange("p j (m t) -> p m t j", t=PACK),
-            )
+            target = grouped[:].rearrange("p (t m j) -> p m t j", t=PACK, j=PACK)
+            source = w1_raw[a, b][:].rearrange("p j (m t) -> p m t j", t=PACK)
+            nc.scalar.copy(target[:, :scalar_share], source[:, :scalar_share])
+            if scalar_share < P:
+                nc.vector.tensor_copy(target[:, scalar_share:], source[:, scalar_share:])
             return grouped
 
         def quantize_w1(a, b, grouped):
@@ -110,48 +114,51 @@ def tile_list_squash_ladder_page_kernel(
         v_s = held([P, S], U8, "v_s")
         v2_w = [held([P, S2], U32, f"v2_w{a}") for a in range(PASSES)]
         v2_s = held([P, S2], U8, "v2_s")
-        floor = held([P, PASSES, CHUNK, PACK], BF16, "floor")
+        floor = held([P, PASSES, FLOOR_RUN, PACK], BF16, "floor")
 
         nc.sync.dma_start(idx[:], offs)
-        nc.sync.dma_start(idx2[:], offs2)
         load_w1(0, 0)
-        load_packed_scales(nc.sync, tab_s, tab_scales)
-        load_w1(1, 0)
-        load_packed_scales(nc.sync, tab2_s, tab2_scales)
-        load_words(tab_w[0], tab_words, 0)
-        load_words(tab_w[1], tab_words, 1)
-        nc.sync.dma_start(least_sb[:], least.rearrange("(b p t) -> p b t", b=PASSES, t=PACK))
-        load_w1(0, 1)
+        load_packed_scales(nc.gpsimd, tab_s, tab_scales)
+        load_packed_scales(nc.gpsimd, tab2_s, tab2_scales)
         for q in range(QUADS):
-            nc.sync.dma_start(
+            nc.gpsimd.dma_start(
                 w4_s[32 * q : 32 * q + 4, :, :].bitcast(I32),
                 w4_scales[:, 4 * q : 4 * q + 4, :].rearrange("a r c -> r a c").bitcast(I32),
             )
+        load_w1(1, 0)
+        load_words(tab_w[0], tab_words, 0)
+        load_words(tab_w[1], tab_words, 1)
+        nc.sync.dma_start(idx2[:], offs2)
+        load_w1(0, 1)
         load_w1(1, 1)
-        nc.vector.tensor_copy(v_s[:], tab_s[:].indirect(idx[:]))
-        nc.sync.dma_start(v_s_low[0:112, :].bitcast(I32), v_s[4:116, :].bitcast(I32))
+        nc.sync.dma_start(least_sb[:], least.rearrange("(b p t) -> p b t", b=PASSES, t=PACK))
         load_words(tab2_w[0], tab2_words, 0)
         load_words(tab2_w[1], tab2_words, 1)
+        nc.vector.tensor_copy(v_s[:], tab_s[:].indirect(idx[:]))
+        nc.sync.dma_start(v_s_low[0:112, :].bitcast(I32), v_s[4:116, :].bitcast(I32))
         nc.sync.dma_start(w4_w[:].bitcast(I32), w4_words.rearrange("a p c -> p a c").bitcast(I32))
+        load_last(0, 0)
+        load_page(0)
         nc.sync.dma_start(idx3[:], offs3)
         with nc.allow_non_contiguous_dma(reason="one factor for each partition"):
             nc.sync.dma_start(member_sb[:], member.rearrange("(i p) -> p i", p=P))
-        load_last(0)
-        nc.sync.dma_start(wgo_sb[:], wgo)
-        for i in range(ROW_TILES):
+        load_wgo(0)
+        for i in range(1, ROW_TILES):
+            load_last(i, 0)
             load_page(i)
-        load_last(1)
+        load_wgo(1)
+        for i in range(ROW_TILES):
+            load_last(i, 1)
 
-        quantize_w1(0, 0, round_w1(0, 0, nc.scalar.copy))
-        nc.vector.tensor_copy(v2_s[:], tab2_s[:].indirect(idx2[:]))
-        quantize_w1(1, 0, round_w1(1, 0, nc.scalar.copy))
-        nc.scalar.copy(floor[:], least_sb[:].unsqueeze(2).to_broadcast([P, PASSES, CHUNK, PACK]))
-
+        quantize_w1(0, 0, round_w1(0, 0, P))
+        quantize_w1(1, 0, round_w1(1, 0, P))
         for g in range(HALVES):
             for a in range(PASSES):
                 gather_words(a, g)
-        quantize_w1(0, 1, round_w1(0, 1, nc.scalar.copy))
-        quantize_w1(1, 1, round_w1(1, 1, nc.vector.tensor_copy))
+        quantize_w1(0, 1, round_w1(0, 1, 64))
+        quantize_w1(1, 1, round_w1(1, 1, 40))
+        nc.scalar.copy(floor[:], least_sb[:].unsqueeze(2).to_broadcast([P, PASSES, FLOOR_RUN, PACK]))
+        nc.vector.tensor_copy(v2_s[:], tab2_s[:].indirect(idx2[:]))
         for a in range(PASSES):
             nc.vector.tensor_copy(v2_w[a][:], tab2_w[a][:].bitcast(U32).indirect(idx2[:]))
 
@@ -176,8 +183,9 @@ def tile_list_squash_ladder_page_kernel(
                             stop=(a == PASSES - 1),
                         )
                 nc.scalar.copy(h[:, c, :].rearrange("p (n t) -> p n t", t=PACK), bank[:].rearrange("p t n -> p n t"))
-            floors = floor[:, b, :, :].rearrange("p n t -> p (n t)").unsqueeze(1).to_broadcast([P, CHUNKS, CHUNK * PACK])
-            nc.vector.tensor_tensor(h[:], h[:], floors, MAX)
+            runs = h[:].rearrange("p c (u x) -> p (c u) x", x=FLOOR_RUN * PACK)
+            floors = floor[:, b, :, :].rearrange("p n t -> p (n t)").unsqueeze(1)
+            nc.vector.tensor_tensor(runs, runs, floors.to_broadcast([P, HALF // FLOOR_RUN, FLOOR_RUN * PACK]), MAX)
             h_c[b, g] = held([P, HALF], U32, f"h_c{b}{g}")
             h_s[b, g] = held([P, HALF], U8, f"h_s{b}{g}")
             nc.vector.quantize_mx(
@@ -209,9 +217,9 @@ def tile_list_squash_ladder_page_kernel(
                     stop=(b == PASSES - 1),
                 )
             factor = ring.tile([P, HALF], F32, name="factor", bufs=8)
-            nc.scalar.activation(factor[:], wgo_sb[:, cols], COPY, scale=member_sb[:, i : i + 1])
+            nc.scalar.activation(factor[:], wgo_sb[g][:], COPY, scale=member_sb[:, i : i + 1])
             best = ring.tile([P, HALF], F32, name="best", bufs=4)
-            nc.vector.tensor_tensor(best[:], bank[:], last_sb[g][:, i, :], MAX)
+            nc.vector.tensor_tensor(best[:], bank[:], last_sb[i, g][:], MAX)
             places = idx3[:, LIST_COLS * g : LIST_COLS * (g + 1)]
             nc.vector.tensor_tensor(page[i][:].indirect(places), best[:], factor[:], MULT)
             if g == HALVES - 1:

@@ -1,6 +1,7 @@
 from contextlib import ExitStack
 
 import concourse.mybir as mybir
+from concourse.masks import make_identity
 
 K, H, T, S, S2, T2, T3 = 1024, 1024, 2048, 1024, 512, 2048, 2048
 FLOPS = 2 * K * H * S + 2 * H * S2 * S + 2 * K * S2 * S
@@ -29,6 +30,7 @@ ROW_TILES = S2 // P
 QUADS = 4
 LIST_COLS = HALF // 16
 FLOOR_RUN = 32
+MEMBER_ROW = PASSES
 
 
 def tile_list_squash_ladder_page_kernel(
@@ -56,7 +58,8 @@ def tile_list_squash_ladder_page_kernel(
         w4_s = held([P, PASSES, S2], U8, "w4_s")
         v_s_low = held([P, S], U8, "v_s_low")
         w1_raw = {(a, b): held([P, PACK, PASS], F32, f"w1_raw{a}{b}") for b in range(PASSES) for a in range(PASSES)}
-        least_sb = held([P, PASSES, PACK], F32, "least_sb")
+        vectors = held([P, PASS], F32, "vectors")
+        identity = held([P, P], F32, "identity")
         member_sb = held([P, ROW_TILES], F32, "member_sb")
         wgo_sb = [held([P, HALF], F32, f"wgo{g}") for g in range(HALVES)]
         last_sb = {(i, g): held([P, HALF], F32, f"last{i}{g}") for g in range(HALVES) for i in range(ROW_TILES)}
@@ -64,13 +67,15 @@ def tile_list_squash_ladder_page_kernel(
 
         for plane in (tab_s, tab2_s, w4_s, v_s_low):
             nc.vector.memset(plane[:].bitcast(I32), 0)
+        nc.gpsimd.memset(vectors[:], 0.0)
+        make_identity(nc, identity[:])
 
         def load_words(tile, words, a):
             nc.sync.dma_start(tile[:], words[a].rearrange("p t i -> p (t i)").bitcast(I32))
 
-        def load_packed_scales(queue, tile, scales):
+        def load_packed_scales(tile, scales):
             for q in range(QUADS):
-                queue.dma_start(
+                nc.sync.dma_start(
                     tile[32 * q : 32 * q + 4 * PASSES, :].bitcast(I32),
                     scales[:, 4 * q : 4 * q + 4, :].bitcast(I32),
                 )
@@ -118,30 +123,29 @@ def tile_list_squash_ladder_page_kernel(
 
         nc.sync.dma_start(idx[:], offs)
         load_w1(0, 0)
-        load_packed_scales(nc.gpsimd, tab_s, tab_scales)
-        load_packed_scales(nc.gpsimd, tab2_s, tab2_scales)
-        for q in range(QUADS):
-            nc.gpsimd.dma_start(
-                w4_s[32 * q : 32 * q + 4, :, :].bitcast(I32),
-                w4_scales[:, 4 * q : 4 * q + 4, :].rearrange("a r c -> r a c").bitcast(I32),
-            )
+        load_packed_scales(tab_s, tab_scales)
+        nc.sync.dma_start(vectors[0:PASSES, :], least.rearrange("(b r) -> b r", b=PASSES))
+        nc.sync.dma_start(vectors[MEMBER_ROW : MEMBER_ROW + ROW_TILES, 0:P], member.rearrange("(i p) -> i p", p=P))
         load_w1(1, 0)
         load_words(tab_w[0], tab_words, 0)
         load_words(tab_w[1], tab_words, 1)
-        nc.sync.dma_start(idx2[:], offs2)
         load_w1(0, 1)
         load_w1(1, 1)
-        nc.sync.dma_start(least_sb[:], least.rearrange("(b p t) -> p b t", b=PASSES, t=PACK))
+        nc.sync.dma_start(idx2[:], offs2)
+        load_packed_scales(tab2_s, tab2_scales)
         load_words(tab2_w[0], tab2_words, 0)
         load_words(tab2_w[1], tab2_words, 1)
         nc.vector.tensor_copy(v_s[:], tab_s[:].indirect(idx[:]))
         nc.sync.dma_start(v_s_low[0:112, :].bitcast(I32), v_s[4:116, :].bitcast(I32))
+        for q in range(QUADS):
+            nc.sync.dma_start(
+                w4_s[32 * q : 32 * q + 4, :, :].bitcast(I32),
+                w4_scales[:, 4 * q : 4 * q + 4, :].rearrange("a r c -> r a c").bitcast(I32),
+            )
         nc.sync.dma_start(w4_w[:].bitcast(I32), w4_words.rearrange("a p c -> p a c").bitcast(I32))
         load_last(0, 0)
         load_page(0)
         nc.sync.dma_start(idx3[:], offs3)
-        with nc.allow_non_contiguous_dma(reason="one factor for each partition"):
-            nc.sync.dma_start(member_sb[:], member.rearrange("(i p) -> p i", p=P))
         load_wgo(0)
         for i in range(1, ROW_TILES):
             load_last(i, 0)
@@ -152,12 +156,21 @@ def tile_list_squash_ladder_page_kernel(
 
         quantize_w1(0, 0, round_w1(0, 0, P))
         quantize_w1(1, 0, round_w1(1, 0, P))
+        turned_least = psum_e.tile([P, PACK, P], F32, name="bank_e")
+        for t in range(PACK):
+            nc.tensor.transpose(turned_least[:, t, :], vectors[:, t:PASS:PACK], identity[:])
+        turned_member = psum_e.tile([P, P], F32, name="bank_e")
+        nc.tensor.transpose(turned_member[:], vectors[:, 0:P], identity[:])
+        nc.scalar.copy(
+            floor[:],
+            turned_least[:, :, 0:PASSES].rearrange("p t b -> p b t").unsqueeze(2).to_broadcast([P, PASSES, FLOOR_RUN, PACK]),
+        )
+        nc.scalar.copy(member_sb[:], turned_member[:, MEMBER_ROW : MEMBER_ROW + ROW_TILES])
         for g in range(HALVES):
             for a in range(PASSES):
                 gather_words(a, g)
         quantize_w1(0, 1, round_w1(0, 1, 64))
         quantize_w1(1, 1, round_w1(1, 1, 40))
-        nc.scalar.copy(floor[:], least_sb[:].unsqueeze(2).to_broadcast([P, PASSES, FLOOR_RUN, PACK]))
         nc.vector.tensor_copy(v2_s[:], tab2_s[:].indirect(idx2[:]))
         for a in range(PASSES):
             nc.vector.tensor_copy(v2_w[a][:], tab2_w[a][:].bitcast(U32).indirect(idx2[:]))

@@ -41,8 +41,8 @@ def tile_list_squash_ladder_page_kernel(
     with ExitStack() as ctx:
         keep = ctx.enter_context(tc.tile_pool(name="keep", bufs=1))
         ring = ctx.enter_context(tc.tile_pool(name="ring", bufs=2))
-        psum_h = ctx.enter_context(tc.psum_pool(name="psum_h", bufs=6))
-        psum_e = ctx.enter_context(tc.psum_pool(name="psum_e", bufs=2))
+        psum_h = ctx.enter_context(tc.psum_pool(name="psum_h", bufs=5))
+        psum_e = ctx.enter_context(tc.psum_pool(name="psum_e", bufs=3))
 
         def held(shape, dtype, name, tag=""):
             return keep.tile(shape, dtype, name=name, tag=tag or name, align_bytes=64)
@@ -62,7 +62,8 @@ def tile_list_squash_ladder_page_kernel(
         identity = held([P, P], F32, "identity")
         member_sb = held([P, ROW_TILES], F32, "member_sb")
         wgo_sb = [held([P, HALF], F32, f"wgo{g}") for g in range(HALVES)]
-        last_sb = {(i, g): held([P, HALF], F32, f"last{i}{g}") for g in range(HALVES) for i in range(ROW_TILES)}
+        last_first = [held([P, HALF], F32, f"last_first{i}") for i in range(ROW_TILES)]
+        last_second = held([P, ROW_TILES, HALF], F32, "last_second")
         page = [held([P, T2], F32, f"page{i}") for i in range(ROW_TILES)]
 
         for plane in (tab_s, tab2_s, w4_s, v_s_low):
@@ -84,8 +85,8 @@ def tile_list_squash_ladder_page_kernel(
             rows = w1[PASS * a : PASS * (a + 1), PASS * b : PASS * (b + 1)]
             nc.sync.dma_start(w1_raw[a, b][:], rows.rearrange("(p j) r -> p j r", j=PACK))
 
-        def load_last(i, g):
-            nc.sync.dma_start(last_sb[i, g][:], last[P * i : P * (i + 1), HALF * g : HALF * (g + 1)])
+        def load_last_first(i):
+            nc.sync.dma_start(last_first[i][:], last[P * i : P * (i + 1), 0:HALF])
 
         def load_wgo(g):
             nc.sync.dma_start(wgo_sb[g][:], wgo[:, HALF * g : HALF * (g + 1)])
@@ -143,16 +144,15 @@ def tile_list_squash_ladder_page_kernel(
                 w4_scales[:, 4 * q : 4 * q + 4, :].rearrange("a r c -> r a c").bitcast(I32),
             )
         nc.sync.dma_start(w4_w[:].bitcast(I32), w4_words.rearrange("a p c -> p a c").bitcast(I32))
-        load_last(0, 0)
-        load_page(0)
+        load_last_first(0)
         nc.sync.dma_start(idx3[:], offs3)
         load_wgo(0)
-        for i in range(1, ROW_TILES):
-            load_last(i, 0)
+        for i in range(ROW_TILES):
+            if i + 1 < ROW_TILES:
+                load_last_first(i + 1)
             load_page(i)
         load_wgo(1)
-        for i in range(ROW_TILES):
-            load_last(i, 1)
+        nc.sync.dma_start(last_second[:], last[:, HALF:S].rearrange("(i p) j -> p i j", p=P))
 
         quantize_w1(0, 0, round_w1(0, 0, P))
         quantize_w1(1, 0, round_w1(1, 0, P))
@@ -205,7 +205,7 @@ def tile_list_squash_ladder_page_kernel(
                 out=h_c[b, g][:].bitcast(FP8X4), scales=h_s[b, g][:], in_=h[:].rearrange("p c x -> p (c x)")
             )
 
-        def place_scores(i, g):
+        def best_scores(i, g):
             cols = slice(HALF * g, HALF * (g + 1))
             rows = slice(P * i, P * (i + 1))
             bank = psum_e.tile([P, HALF], F32, name="bank_e")
@@ -229,17 +229,24 @@ def tile_list_squash_ladder_page_kernel(
                     start=False,
                     stop=(b == PASSES - 1),
                 )
+            best = ring.tile([P, HALF], F32, name="best", bufs=4)
+            last_cols = last_first[i][:] if g == 0 else last_second[:, i, :]
+            nc.vector.tensor_tensor(best[:], bank[:], last_cols, MAX)
+            return best
+
+        def place(i, g, best):
             factor = ring.tile([P, HALF], F32, name="factor", bufs=8)
             nc.scalar.activation(factor[:], wgo_sb[g][:], COPY, scale=member_sb[:, i : i + 1])
-            best = ring.tile([P, HALF], F32, name="best", bufs=4)
-            nc.vector.tensor_tensor(best[:], bank[:], last_sb[i, g][:], MAX)
             places = idx3[:, LIST_COLS * g : LIST_COLS * (g + 1)]
             nc.vector.tensor_tensor(page[i][:].indirect(places), best[:], factor[:], MULT)
             if g == HALVES - 1:
-                nc.sync.dma_start(out[rows, :], page[i][:])
+                nc.sync.dma_start(out[P * i : P * (i + 1), :], page[i][:])
 
         for g in range(HALVES):
             for b in range(PASSES):
                 features(b, g)
+            best = best_scores(0, g)
             for i in range(ROW_TILES):
-                place_scores(i, g)
+                ahead = best_scores(i + 1, g) if i + 1 < ROW_TILES else None
+                place(i, g, best)
+                best = ahead

from contextlib import ExitStack

import concourse.mybir as mybir
from concourse.masks import make_identity

K, H, T, S, S2, T2, T3 = 1024, 1024, 2048, 1024, 512, 2048, 2048
FLOPS = 2 * K * H * S + 2 * H * S2 * S + 2 * K * S2 * S

F32 = mybir.dt.float32
BF16 = mybir.dt.bfloat16
I32 = mybir.dt.int32
U32 = mybir.dt.uint32
U16 = mybir.dt.uint16
U8 = mybir.dt.uint8
FP8X4 = mybir.dt.float8_e4m3fn_x4
FP4X4 = mybir.dt.float4_e2m1fn_x4
MAX = mybir.AluOpType.max
MULT = mybir.AluOpType.mult
COPY = mybir.ActivationFunctionType.Copy

P = 128
PACK = 4
PASS = P * PACK
PASSES = 2
HALF = 512
HALVES = S // HALF
CHUNK = 128
CHUNKS = HALF // CHUNK
ROW_TILES = S2 // P
QUADS = 4
LIST_COLS = HALF // 16
FLOOR_RUN = 32
MEMBER_ROW = PASSES


def tile_list_squash_ladder_page_kernel(
    tc, tab_words, tab_scales, tab2_words, tab2_scales, w4_words, w4_scales,
    w1, least, last, member, page1, wgo, offs, offs2, offs3, out,
):
    nc = tc.nc
    with ExitStack() as ctx:
        keep = ctx.enter_context(tc.tile_pool(name="keep", bufs=1))
        ring = ctx.enter_context(tc.tile_pool(name="ring", bufs=2))
        psum_h = ctx.enter_context(tc.psum_pool(name="psum_h", bufs=5))
        psum_e = ctx.enter_context(tc.psum_pool(name="psum_e", bufs=3))

        def held(shape, dtype, name, tag=""):
            return keep.tile(shape, dtype, name=name, tag=tag or name, align_bytes=64)

        idx = held([P, S // 16], U16, "idx")
        idx2 = held([P, S2 // 16], U16, "idx2")
        idx3 = held([P, S // 16], U16, "idx3")
        tab_w = [held([P, T], I32, f"tab_w{a}") for a in range(PASSES)]
        tab2_w = [held([P, T3], I32, f"tab2_w{a}") for a in range(PASSES)]
        tab_s = held([P, T], U8, "tab_s")
        tab2_s = held([P, T3], U8, "tab2_s")
        w4_w = held([P, PASSES, 2 * S2], U8, "w4_w")
        w4_s = held([P, PASSES, S2], U8, "w4_s")
        v_s_low = held([P, S], U8, "v_s_low")
        w1_raw = {(a, b): held([P, PACK, PASS], F32, f"w1_raw{a}{b}") for b in range(PASSES) for a in range(PASSES)}
        vectors = held([P, PASS], F32, "vectors")
        identity = held([P, P], F32, "identity")
        member_sb = held([P, ROW_TILES], F32, "member_sb")
        wgo_sb = [held([P, HALF], F32, f"wgo{g}") for g in range(HALVES)]
        last_first = [held([P, HALF], F32, f"last_first{i}") for i in range(ROW_TILES)]
        last_second = held([P, ROW_TILES, HALF], F32, "last_second")
        page = [held([P, T2], F32, f"page{i}") for i in range(ROW_TILES)]

        for plane in (tab_s, tab2_s, w4_s, v_s_low):
            nc.vector.memset(plane[:].bitcast(I32), 0)
        nc.gpsimd.memset(vectors[:], 0.0)
        make_identity(nc, identity[:])

        def load_words(tile, words, a):
            nc.sync.dma_start(tile[:], words[a].rearrange("p t i -> p (t i)").bitcast(I32))

        def load_packed_scales(tile, scales):
            for q in range(QUADS):
                nc.sync.dma_start(
                    tile[32 * q : 32 * q + 4 * PASSES, :].bitcast(I32),
                    scales[:, 4 * q : 4 * q + 4, :].bitcast(I32),
                )

        def load_w1(a, b):
            rows = w1[PASS * a : PASS * (a + 1), PASS * b : PASS * (b + 1)]
            nc.sync.dma_start(w1_raw[a, b][:], rows.rearrange("(p j) r -> p j r", j=PACK))

        def load_last_first(i):
            nc.sync.dma_start(last_first[i][:], last[P * i : P * (i + 1), 0:HALF])

        def load_wgo(g):
            nc.sync.dma_start(wgo_sb[g][:], wgo[:, HALF * g : HALF * (g + 1)])

        def load_page(i):
            nc.sync.dma_start(page[i][:], page1[P * i : P * (i + 1), :])

        v_w = {}

        def gather_words(a, g):
            v_w[a, g] = held([P, HALF], U32, f"v_w{a}{g}")
            entries = idx[:, LIST_COLS * g : LIST_COLS * (g + 1)]
            nc.vector.tensor_copy(v_w[a, g][:], tab_w[a][:].bitcast(U32).indirect(entries))

        w1_c, w1_s = {}, {}

        def round_w1(a, b, scalar_share):
            grouped = ring.tile([P, PASS * PACK], BF16, name="w1_grouped", align_bytes=64, bufs=4)
            target = grouped[:].rearrange("p (t m j) -> p m t j", t=PACK, j=PACK)
            source = w1_raw[a, b][:].rearrange("p j (m t) -> p m t j", t=PACK)
            nc.scalar.copy(target[:, :scalar_share], source[:, :scalar_share])
            if scalar_share < P:
                nc.vector.tensor_copy(target[:, scalar_share:], source[:, scalar_share:])
            return grouped

        def quantize_w1(a, b, grouped):
            w1_c[a, b] = held([P, PASS], U32, f"w1_c{a}{b}")
            w1_s[a, b] = held([P, PASS], U8, f"w1_s{a}{b}")
            nc.vector.quantize_mx(out=w1_c[a, b][:].bitcast(FP8X4), scales=w1_s[a, b][:], in_=grouped[:])

        v_s = held([P, S], U8, "v_s")
        v2_w = [held([P, S2], U32, f"v2_w{a}") for a in range(PASSES)]
        v2_s = held([P, S2], U8, "v2_s")
        floor = held([P, PASSES, FLOOR_RUN, PACK], BF16, "floor")

        nc.sync.dma_start(idx[:], offs)
        load_w1(0, 0)
        load_packed_scales(tab_s, tab_scales)
        nc.sync.dma_start(vectors[0:PASSES, :], least.rearrange("(b r) -> b r", b=PASSES))
        nc.sync.dma_start(vectors[MEMBER_ROW : MEMBER_ROW + ROW_TILES, 0:P], member.rearrange("(i p) -> i p", p=P))
        load_w1(1, 0)
        load_words(tab_w[0], tab_words, 0)
        load_words(tab_w[1], tab_words, 1)
        load_w1(0, 1)
        load_w1(1, 1)
        nc.sync.dma_start(idx2[:], offs2)
        load_packed_scales(tab2_s, tab2_scales)
        load_words(tab2_w[0], tab2_words, 0)
        load_words(tab2_w[1], tab2_words, 1)
        nc.vector.tensor_copy(v_s[:], tab_s[:].indirect(idx[:]))
        nc.sync.dma_start(v_s_low[0:112, :].bitcast(I32), v_s[4:116, :].bitcast(I32))
        for q in range(QUADS):
            nc.sync.dma_start(
                w4_s[32 * q : 32 * q + 4, :, :].bitcast(I32),
                w4_scales[:, 4 * q : 4 * q + 4, :].rearrange("a r c -> r a c").bitcast(I32),
            )
        nc.sync.dma_start(w4_w[:].bitcast(I32), w4_words.rearrange("a p c -> p a c").bitcast(I32))
        load_last_first(0)
        nc.sync.dma_start(idx3[:], offs3)
        load_wgo(0)
        for i in range(ROW_TILES):
            if i + 1 < ROW_TILES:
                load_last_first(i + 1)
            load_page(i)
        load_wgo(1)
        nc.sync.dma_start(last_second[:], last[:, HALF:S].rearrange("(i p) j -> p i j", p=P))

        quantize_w1(0, 0, round_w1(0, 0, P))
        quantize_w1(1, 0, round_w1(1, 0, P))
        turned_least = psum_e.tile([P, PACK, P], F32, name="bank_e")
        for t in range(PACK):
            nc.tensor.transpose(turned_least[:, t, :], vectors[:, t:PASS:PACK], identity[:])
        turned_member = psum_e.tile([P, P], F32, name="bank_e")
        nc.tensor.transpose(turned_member[:], vectors[:, 0:P], identity[:])
        nc.scalar.copy(
            floor[:],
            turned_least[:, :, 0:PASSES].rearrange("p t b -> p b t").unsqueeze(2).to_broadcast([P, PASSES, FLOOR_RUN, PACK]),
        )
        nc.scalar.copy(member_sb[:], turned_member[:, MEMBER_ROW : MEMBER_ROW + ROW_TILES])
        for g in range(HALVES):
            for a in range(PASSES):
                gather_words(a, g)
        quantize_w1(0, 1, round_w1(0, 1, 64))
        quantize_w1(1, 1, round_w1(1, 1, 40))
        nc.vector.tensor_copy(v2_s[:], tab2_s[:].indirect(idx2[:]))
        for a in range(PASSES):
            nc.vector.tensor_copy(v2_w[a][:], tab2_w[a][:].bitcast(U32).indirect(idx2[:]))

        h_c, h_s = {}, {}

        def features(b, g):
            h = held([P, CHUNKS, CHUNK * PACK], BF16, f"h{b}{g}", tag="w1_raw11" if (b, g) == (0, 0) else "")
            for c in range(CHUNKS):
                bank = psum_h.tile([P, PACK, CHUNK], F32, name="bank_h")
                cols = slice(CHUNK * c, CHUNK * (c + 1))
                list_cols = slice(HALF * g + CHUNK * c, HALF * g + CHUNK * (c + 1))
                for t in range(PACK):
                    slot = slice(P * t, P * (t + 1))
                    for a in range(PASSES):
                        nc.tensor.matmul_mx(
                            out=bank[:, t, :],
                            lhsT=w1_c[a, b][:, slot].bitcast(FP8X4),
                            lhsT_scale=w1_s[a, b][:, slot],
                            rhs=v_w[a, g][:, cols].bitcast(FP8X4),
                            rhs_scale=v_s[4 * a : P, list_cols],
                            start=(a == 0),
                            stop=(a == PASSES - 1),
                        )
                nc.scalar.copy(h[:, c, :].rearrange("p (n t) -> p n t", t=PACK), bank[:].rearrange("p t n -> p n t"))
            runs = h[:].rearrange("p c (u x) -> p (c u) x", x=FLOOR_RUN * PACK)
            floors = floor[:, b, :, :].rearrange("p n t -> p (n t)").unsqueeze(1)
            nc.vector.tensor_tensor(runs, runs, floors.to_broadcast([P, HALF // FLOOR_RUN, FLOOR_RUN * PACK]), MAX)
            h_c[b, g] = held([P, HALF], U32, f"h_c{b}{g}")
            h_s[b, g] = held([P, HALF], U8, f"h_s{b}{g}")
            nc.vector.quantize_mx(
                out=h_c[b, g][:].bitcast(FP8X4), scales=h_s[b, g][:], in_=h[:].rearrange("p c x -> p (c x)")
            )

        def best_scores(i, g):
            cols = slice(HALF * g, HALF * (g + 1))
            rows = slice(P * i, P * (i + 1))
            bank = psum_e.tile([P, HALF], F32, name="bank_e")
            for a in range(PASSES):
                nc.tensor.matmul_mx(
                    out=bank[:],
                    lhsT=w4_w[:, a, 2 * P * i : 2 * P * (i + 1)].bitcast(FP4X4),
                    lhsT_scale=w4_s[:, a, rows],
                    rhs=v_w[a, g][:].bitcast(FP8X4),
                    rhs_scale=(v_s, v_s_low)[a][:, cols],
                    start=(a == 0),
                    stop=False,
                )
            for b in range(PASSES):
                nc.tensor.matmul_mx(
                    out=bank[:],
                    lhsT=v2_w[b][:, rows].bitcast(FP8X4),
                    lhsT_scale=v2_s[4 * b : P, rows],
                    rhs=h_c[b, g][:].bitcast(FP8X4),
                    rhs_scale=h_s[b, g][:],
                    start=False,
                    stop=(b == PASSES - 1),
                )
            best = ring.tile([P, HALF], F32, name="best", bufs=4)
            last_cols = last_first[i][:] if g == 0 else last_second[:, i, :]
            nc.vector.tensor_tensor(best[:], bank[:], last_cols, MAX)
            return best

        def place(i, g, best):
            factor = ring.tile([P, HALF], F32, name="factor", bufs=8)
            nc.scalar.activation(factor[:], wgo_sb[g][:], COPY, scale=member_sb[:, i : i + 1])
            places = idx3[:, LIST_COLS * g : LIST_COLS * (g + 1)]
            nc.vector.tensor_tensor(page[i][:].indirect(places), best[:], factor[:], MULT)
            if g == HALVES - 1:
                nc.sync.dma_start(out[P * i : P * (i + 1), :], page[i][:])

        for g in range(HALVES):
            for b in range(PASSES):
                features(b, g)
            best = best_scores(0, g)
            for i in range(ROW_TILES):
                ahead = best_scores(i + 1, g) if i + 1 < ROW_TILES else None
                place(i, g, best)
                best = ahead
